import numpy as np
CORES = [14,30,46,62,78,94,110,126,6,22,38,54,70,86,102,118]
N = 16
T, K = 256, 1
ROUTE = [[[3],[15],[4],[2],[11],[11],[0],[8],[11],[7],[7],[4],[8],[9],[5],[1],[4],[3],[7],[8],[9],[4],[13],[1],[7],[9],[7],[13],[0],[9],[3],[9],[5],[1],[6],[4],[4],[14],[6],[12],[10],[4],[8],[13],[11],[7],[3],[13],[10],[15],[1],[10],[6],[1],[8],[9],[2],[0],[10],[0],[5],[11],[1],[15],[7],[15],[1],[10],[15],[14],[11],[2],[11],[10],[5],[3],[13],[2],[6],[2],[14],[7],[6],[10],[3],[2],[7],[5],[7],[11],[3],[4],[10],[13],[15],[5],[8],[8],[10],[6],[8],[9],[0],[12],[1],[12],[3],[1],[13],[8],[1],[11],[15],[5],[9],[4],[5],[8],[2],[11],[0],[14],[15],[1],[2],[4],[15],[13],[0],[5],[10],[15],[3],[0],[6],[0],[3],[8],[11],[8],[6],[0],[2],[3],[10],[6],[12],[14],[4],[5],[6],[9],[13],[9],[11],[5],[8],[15],[13],[11],[8],[1],[9],[14],[9],[8],[10],[10],[10],[2],[15],[3],[13],[14],[11],[12],[8],[6],[1],[4],[15],[4],[14],[1],[14],[9],[9],[6],[15],[3],[1],[3],[3],[11],[4],[7],[9],[5],[3],[15],[5],[8],[4],[12],[5],[5],[3],[10],[3],[2],[5],[0],[1],[7],[9],[11],[1],[1],[11],[8],[8],[6],[15],[2],[9],[9],[0],[1],[7],[8],[5],[10],[0],[14],[11],[8],[7],[6],[12],[8],[11],[12],[14],[11],[6],[3],[8],[10],[3],[11],[15],[12],[1],[10],[15],[3]],[[10],[1],[15],[3],[14],[15],[12],[5],[1],[13],[8],[6],[3],[0],[5],[5],[14],[6],[4],[5],[11],[10],[11],[7],[0],[12],[0],[0],[12],[2],[1],[1],[0],[7],[15],[8],[14],[13],[9],[11],[10],[4],[14],[7],[15],[6],[3],[13],[15],[11],[7],[10],[2],[2],[2],[1],[8],[4],[3],[15],[12],[10],[11],[15],[3],[6],[7],[5],[6],[6],[14],[4],[11],[10],[1],[10],[13],[0],[10],[2],[15],[2],[5],[13],[11],[12],[2],[6],[3],[5],[5],[1],[9],[6],[2],[14],[9],[8],[14],[14],[2],[1],[9],[8],[12],[4],[9],[9],[12],[15],[5],[0],[5],[2],[9],[10],[11],[12],[2],[15],[3],[10],[9],[5],[6],[14],[0],[8],[1],[4],[9],[3],[9],[8],[6],[0],[12],[2],[12],[1],[2],[2],[10],[5],[7],[15],[8],[2],[4],[2],[1],[7],[3],[15],[10],[15],[3],[4],[6],[6],[8],[5],[1],[6],[9],[7],[13],[5],[11],[6],[5],[7],[1],[9],[6],[0],[3],[11],[0],[13],[2],[11],[5],[10],[15],[13],[10],[15],[15],[8],[13],[12],[4],[4],[13],[11],[12],[3],[2],[13],[13],[11],[3],[15],[6],[5],[0],[4],[15],[3],[7],[6],[2],[14],[11],[14],[0],[4],[14],[14],[5],[1],[1],[13],[4],[6],[14],[11],[11],[4],[11],[1],[12],[11],[13],[5],[14],[3],[11],[15],[5],[12],[6],[0],[5],[0],[8],[9],[8],[2],[8],[9],[15],[3],[5],[1]],[[12],[1],[13],[10],[10],[12],[9],[4],[0],[3],[6],[3],[15],[15],[8],[9],[0],[14],[9],[8],[6],[14],[2],[15],[14],[15],[5],[11],[1],[3],[0],[9],[11],[1],[5],[10],[9],[7],[13],[12],[8],[6],[2],[11],[9],[7],[9],[1],[15],[14],[10],[4],[5],[13],[5],[1],[1],[0],[12],[7],[5],[1],[8],[10],[7],[1],[9],[6],[4],[8],[12],[3],[7],[5],[6],[2],[14],[11],[15],[1],[12],[13],[7],[2],[6],[9],[3],[7],[0],[9],[11],[5],[12],[11],[3],[8],[0],[15],[7],[7],[6],[2],[2],[2],[1],[6],[6],[1],[1],[3],[13],[0],[15],[1],[7],[5],[8],[6],[11],[15],[3],[3],[1],[5],[6],[14],[8],[7],[14],[3],[7],[7],[10],[5],[6],[8],[5],[4],[8],[3],[3],[4],[6],[7],[8],[8],[1],[2],[4],[8],[0],[3],[5],[9],[0],[6],[2],[6],[4],[6],[9],[0],[12],[5],[3],[11],[0],[14],[7],[9],[7],[6],[8],[5],[6],[15],[6],[6],[11],[1],[0],[0],[7],[10],[3],[1],[14],[4],[13],[0],[1],[4],[7],[12],[15],[13],[4],[0],[11],[2],[15],[0],[13],[4],[11],[12],[13],[7],[12],[15],[0],[15],[1],[10],[13],[14],[11],[12],[9],[10],[7],[4],[5],[2],[2],[9],[2],[2],[7],[4],[13],[0],[1],[4],[2],[2],[14],[0],[2],[14],[0],[12],[6],[5],[5],[12],[12],[10],[6],[12],[2],[0],[3],[6],[1],[11]],[[0],[0],[10],[15],[8],[11],[15],[0],[13],[9],[8],[0],[2],[6],[13],[3],[1],[6],[11],[1],[13],[0],[13],[5],[15],[0],[3],[11],[6],[8],[0],[1],[0],[6],[3],[2],[7],[6],[8],[11],[0],[6],[4],[1],[7],[1],[1],[2],[14],[1],[11],[15],[7],[7],[9],[2],[2],[4],[5],[9],[11],[15],[10],[14],[6],[10],[12],[13],[0],[4],[5],[2],[4],[0],[0],[13],[2],[7],[1],[8],[12],[10],[3],[10],[4],[15],[10],[7],[7],[0],[13],[0],[9],[3],[13],[13],[9],[0],[14],[11],[12],[7],[14],[13],[4],[9],[13],[12],[6],[2],[5],[11],[15],[15],[11],[2],[0],[11],[11],[7],[9],[0],[8],[14],[9],[6],[12],[6],[8],[7],[13],[4],[5],[13],[10],[12],[15],[13],[6],[10],[3],[7],[15],[14],[14],[6],[14],[6],[7],[14],[2],[10],[0],[10],[13],[9],[12],[9],[8],[3],[5],[0],[9],[15],[5],[12],[1],[5],[4],[15],[1],[13],[6],[15],[8],[4],[12],[9],[13],[1],[5],[1],[6],[2],[15],[11],[0],[7],[4],[14],[15],[2],[2],[6],[14],[14],[6],[9],[4],[1],[6],[10],[7],[7],[11],[1],[1],[6],[7],[3],[2],[14],[2],[2],[4],[7],[12],[6],[14],[2],[3],[4],[1],[4],[6],[3],[14],[5],[2],[12],[5],[11],[6],[2],[11],[2],[1],[11],[10],[5],[15],[3],[15],[13],[13],[14],[5],[5],[8],[6],[4],[9],[6],[0],[12],[7]],[[12],[14],[0],[14],[12],[15],[5],[14],[6],[8],[8],[9],[7],[11],[9],[15],[3],[5],[10],[3],[5],[14],[15],[14],[15],[10],[13],[10],[0],[9],[0],[6],[10],[10],[0],[13],[14],[11],[0],[1],[0],[10],[15],[8],[5],[5],[0],[9],[6],[10],[13],[7],[5],[15],[11],[9],[8],[2],[11],[12],[13],[4],[1],[1],[11],[8],[12],[14],[11],[2],[4],[4],[6],[10],[15],[13],[1],[9],[2],[13],[11],[13],[13],[11],[2],[8],[8],[4],[0],[0],[4],[8],[2],[0],[9],[11],[12],[14],[12],[0],[14],[9],[3],[7],[0],[7],[0],[0],[2],[5],[5],[5],[0],[14],[2],[1],[6],[11],[7],[5],[0],[2],[11],[11],[12],[8],[6],[0],[7],[13],[3],[9],[8],[8],[9],[5],[10],[9],[13],[8],[1],[7],[1],[12],[12],[3],[3],[9],[12],[0],[1],[8],[14],[1],[7],[0],[4],[9],[12],[11],[11],[7],[14],[15],[5],[4],[15],[15],[1],[8],[5],[11],[4],[4],[6],[13],[10],[8],[10],[6],[6],[15],[0],[8],[3],[15],[15],[11],[13],[9],[8],[1],[2],[15],[12],[11],[7],[4],[15],[8],[10],[14],[10],[1],[0],[3],[11],[15],[0],[9],[15],[6],[7],[5],[15],[9],[6],[0],[5],[11],[6],[7],[11],[3],[10],[0],[12],[10],[9],[9],[2],[8],[2],[2],[3],[2],[5],[14],[6],[0],[5],[3],[13],[15],[14],[11],[3],[10],[14],[14],[5],[14],[9],[1],[3],[5]],[[9],[15],[12],[14],[6],[3],[12],[12],[3],[6],[15],[13],[3],[14],[9],[4],[0],[3],[8],[0],[12],[10],[10],[1],[1],[2],[8],[12],[0],[7],[11],[0],[2],[7],[13],[3],[6],[1],[4],[10],[0],[2],[2],[13],[11],[5],[6],[2],[2],[13],[7],[12],[5],[1],[6],[7],[6],[0],[13],[14],[14],[2],[14],[4],[2],[9],[15],[3],[2],[1],[4],[2],[9],[0],[8],[5],[3],[3],[10],[2],[13],[4],[0],[9],[5],[10],[11],[4],[14],[1],[2],[7],[1],[2],[4],[0],[5],[6],[2],[9],[7],[1],[7],[12],[8],[11],[12],[10],[4],[14],[13],[13],[11],[2],[5],[10],[15],[10],[10],[1],[6],[7],[3],[4],[1],[6],[6],[10],[1],[12],[15],[10],[15],[0],[0],[15],[0],[12],[5],[7],[7],[0],[7],[1],[2],[6],[15],[6],[1],[12],[3],[12],[12],[11],[1],[14],[0],[0],[13],[1],[15],[8],[8],[0],[9],[13],[5],[9],[7],[15],[13],[11],[15],[1],[0],[10],[11],[10],[0],[15],[12],[4],[1],[11],[5],[13],[15],[8],[9],[11],[14],[12],[8],[8],[6],[3],[9],[9],[10],[6],[4],[15],[8],[14],[1],[12],[0],[7],[10],[10],[13],[4],[11],[6],[12],[13],[9],[9],[7],[14],[6],[7],[14],[13],[9],[12],[5],[14],[6],[0],[5],[9],[8],[15],[1],[14],[1],[9],[7],[13],[11],[12],[13],[2],[1],[0],[13],[14],[6],[5],[3],[6],[14],[11],[0],[10]],[[8],[3],[2],[13],[4],[15],[8],[1],[9],[3],[13],[15],[2],[4],[6],[12],[14],[8],[11],[3],[3],[10],[14],[7],[10],[13],[6],[9],[11],[2],[12],[9],[6],[5],[7],[4],[5],[8],[15],[8],[5],[6],[10],[1],[10],[10],[13],[7],[13],[4],[11],[8],[10],[6],[4],[8],[4],[1],[14],[5],[2],[13],[4],[15],[2],[11],[10],[1],[12],[12],[2],[9],[1],[7],[11],[5],[0],[4],[4],[8],[9],[8],[12],[9],[13],[13],[11],[15],[1],[2],[11],[6],[5],[15],[2],[3],[4],[15],[8],[11],[5],[10],[15],[3],[11],[3],[13],[14],[10],[15],[10],[0],[14],[3],[7],[6],[7],[15],[12],[0],[11],[6],[12],[5],[0],[10],[13],[11],[1],[8],[4],[4],[8],[4],[2],[9],[7],[5],[7],[10],[0],[5],[12],[11],[13],[13],[10],[12],[2],[1],[6],[1],[6],[15],[9],[4],[7],[5],[15],[4],[5],[12],[13],[7],[11],[7],[7],[11],[4],[7],[3],[13],[5],[14],[5],[1],[13],[8],[5],[5],[4],[12],[13],[6],[15],[15],[2],[14],[2],[6],[2],[4],[13],[11],[4],[10],[7],[10],[7],[15],[7],[6],[6],[7],[6],[11],[10],[7],[14],[3],[8],[8],[8],[15],[3],[5],[6],[3],[3],[2],[2],[8],[11],[9],[14],[9],[10],[3],[14],[9],[13],[9],[3],[15],[8],[4],[8],[8],[15],[10],[12],[6],[7],[7],[10],[14],[0],[0],[15],[8],[15],[1],[13],[5],[5],[3]],[[1],[13],[8],[12],[11],[14],[9],[1],[0],[15],[2],[3],[3],[4],[9],[2],[7],[9],[10],[1],[1],[13],[9],[6],[15],[15],[14],[7],[7],[5],[3],[5],[3],[14],[7],[9],[4],[12],[13],[13],[7],[12],[7],[1],[11],[14],[5],[14],[3],[13],[2],[4],[8],[2],[13],[2],[11],[13],[7],[5],[2],[2],[7],[8],[7],[13],[11],[7],[0],[2],[8],[10],[7],[7],[12],[15],[5],[9],[3],[4],[7],[12],[1],[7],[13],[15],[10],[9],[0],[6],[2],[11],[6],[12],[1],[7],[10],[8],[11],[1],[8],[1],[8],[9],[11],[3],[6],[2],[1],[3],[8],[0],[13],[0],[13],[7],[3],[11],[4],[7],[3],[0],[14],[2],[6],[3],[4],[3],[10],[3],[14],[9],[3],[12],[10],[6],[12],[14],[0],[13],[6],[13],[5],[6],[7],[10],[8],[14],[2],[3],[6],[12],[5],[10],[4],[2],[4],[14],[15],[15],[12],[9],[12],[7],[13],[10],[12],[8],[11],[15],[15],[12],[12],[1],[1],[4],[2],[10],[13],[14],[9],[3],[2],[13],[10],[11],[13],[6],[15],[10],[8],[13],[13],[7],[8],[6],[12],[13],[8],[10],[4],[15],[13],[5],[4],[3],[14],[12],[14],[2],[8],[3],[6],[12],[9],[15],[15],[15],[13],[0],[12],[3],[4],[4],[12],[10],[8],[1],[13],[4],[1],[13],[10],[13],[12],[15],[7],[5],[13],[9],[15],[8],[15],[6],[11],[9],[13],[11],[2],[6],[0],[14],[7],[13],[4],[2]],[[7],[12],[11],[11],[10],[8],[4],[15],[11],[13],[6],[2],[8],[4],[14],[13],[10],[3],[8],[1],[12],[2],[15],[6],[5],[10],[13],[7],[6],[1],[12],[15],[11],[10],[0],[4],[11],[7],[11],[7],[4],[13],[5],[5],[1],[6],[3],[6],[6],[9],[3],[14],[4],[13],[7],[9],[13],[2],[13],[13],[11],[5],[6],[8],[7],[11],[2],[11],[8],[2],[1],[4],[10],[3],[9],[4],[9],[1],[13],[6],[14],[11],[0],[14],[7],[13],[11],[12],[13],[14],[11],[15],[11],[11],[3],[15],[4],[15],[0],[8],[2],[2],[7],[6],[9],[6],[14],[8],[2],[11],[12],[6],[8],[12],[14],[2],[7],[6],[10],[13],[8],[9],[7],[5],[9],[13],[13],[2],[4],[13],[13],[8],[6],[10],[2],[6],[15],[15],[12],[2],[5],[14],[15],[12],[6],[2],[1],[11],[9],[14],[7],[11],[6],[3],[7],[8],[1],[4],[12],[7],[11],[6],[13],[0],[6],[8],[5],[7],[14],[11],[2],[0],[12],[1],[14],[10],[2],[3],[5],[8],[0],[2],[5],[0],[3],[5],[5],[11],[15],[2],[3],[6],[12],[0],[7],[2],[3],[3],[6],[15],[6],[5],[13],[2],[14],[1],[8],[5],[15],[1],[1],[15],[10],[5],[6],[0],[0],[7],[13],[12],[12],[5],[2],[13],[4],[11],[12],[3],[3],[11],[1],[8],[0],[7],[2],[14],[6],[15],[9],[11],[4],[3],[15],[12],[5],[2],[1],[13],[8],[13],[3],[7],[2],[6],[14],[3]],[[11],[12],[10],[13],[10],[10],[4],[11],[5],[6],[2],[3],[8],[15],[7],[5],[13],[13],[1],[3],[2],[6],[5],[13],[14],[15],[8],[4],[7],[10],[5],[13],[14],[4],[12],[0],[5],[8],[6],[5],[3],[0],[7],[5],[4],[15],[8],[10],[7],[5],[4],[0],[12],[15],[7],[10],[6],[5],[9],[5],[9],[14],[2],[15],[8],[7],[2],[10],[3],[11],[3],[15],[12],[9],[12],[0],[1],[6],[7],[6],[15],[3],[1],[8],[3],[13],[6],[0],[8],[15],[4],[13],[0],[14],[12],[2],[7],[7],[6],[15],[15],[13],[0],[7],[4],[11],[5],[2],[6],[4],[14],[4],[14],[8],[11],[1],[13],[5],[8],[10],[8],[1],[15],[9],[1],[11],[13],[9],[1],[9],[10],[4],[15],[9],[10],[4],[12],[14],[7],[12],[3],[14],[0],[11],[1],[10],[7],[7],[10],[10],[13],[2],[13],[7],[6],[1],[1],[3],[13],[0],[1],[8],[8],[1],[1],[6],[0],[13],[13],[9],[10],[14],[0],[13],[11],[15],[4],[12],[5],[11],[0],[13],[11],[8],[13],[8],[15],[12],[10],[15],[13],[1],[13],[0],[13],[4],[3],[14],[10],[7],[5],[9],[6],[14],[13],[9],[9],[12],[10],[1],[15],[8],[9],[7],[1],[14],[0],[14],[13],[14],[8],[13],[10],[13],[13],[2],[15],[6],[7],[15],[10],[9],[7],[9],[4],[0],[3],[15],[9],[10],[9],[14],[9],[11],[3],[12],[10],[14],[2],[5],[1],[14],[6],[13],[9],[11]],[[14],[14],[6],[15],[3],[4],[11],[8],[0],[2],[4],[0],[8],[2],[4],[12],[5],[4],[13],[1],[4],[0],[14],[14],[3],[8],[4],[5],[8],[9],[7],[3],[10],[7],[10],[6],[0],[10],[0],[8],[13],[5],[13],[5],[14],[5],[5],[1],[0],[1],[4],[11],[6],[5],[14],[2],[8],[10],[0],[10],[1],[10],[9],[12],[14],[2],[5],[0],[14],[7],[6],[0],[6],[6],[1],[8],[10],[7],[10],[13],[14],[4],[6],[8],[3],[12],[2],[15],[1],[13],[4],[15],[12],[4],[13],[15],[14],[9],[15],[14],[14],[1],[2],[2],[3],[4],[1],[2],[14],[3],[3],[15],[14],[8],[12],[11],[0],[15],[14],[11],[8],[14],[3],[12],[14],[13],[4],[4],[1],[6],[13],[0],[0],[9],[1],[11],[7],[15],[2],[5],[11],[4],[11],[11],[4],[11],[13],[4],[5],[7],[12],[1],[12],[8],[8],[11],[9],[5],[11],[8],[2],[14],[9],[13],[4],[9],[6],[6],[7],[2],[7],[0],[7],[5],[0],[0],[10],[7],[10],[5],[6],[2],[2],[0],[12],[0],[1],[9],[0],[6],[9],[6],[5],[8],[15],[6],[11],[10],[10],[9],[8],[9],[15],[6],[11],[12],[11],[5],[5],[14],[9],[13],[6],[2],[8],[10],[4],[5],[4],[0],[7],[4],[1],[0],[0],[14],[8],[9],[4],[0],[10],[4],[8],[8],[1],[7],[8],[0],[0],[1],[5],[2],[9],[10],[15],[1],[3],[12],[7],[9],[13],[15],[11],[7],[1],[12]],[[15],[13],[9],[6],[9],[11],[12],[8],[14],[7],[15],[12],[8],[4],[10],[4],[9],[4],[1],[10],[4],[14],[15],[3],[5],[7],[7],[1],[14],[1],[15],[1],[12],[3],[5],[1],[10],[5],[4],[8],[7],[9],[9],[4],[5],[1],[3],[12],[12],[8],[3],[0],[8],[10],[3],[2],[5],[15],[0],[11],[5],[4],[6],[3],[3],[8],[1],[15],[8],[13],[13],[14],[12],[11],[6],[15],[3],[14],[14],[2],[11],[7],[4],[3],[14],[11],[15],[15],[8],[4],[11],[4],[2],[11],[9],[4],[4],[8],[13],[3],[12],[6],[11],[13],[12],[9],[6],[5],[2],[7],[11],[4],[0],[12],[1],[1],[5],[6],[5],[10],[2],[12],[7],[7],[8],[11],[1],[2],[8],[12],[11],[2],[3],[10],[2],[5],[3],[9],[3],[15],[4],[14],[12],[14],[13],[12],[8],[14],[4],[15],[5],[10],[6],[2],[1],[3],[10],[1],[11],[12],[15],[11],[14],[3],[11],[1],[2],[14],[5],[12],[1],[5],[11],[15],[0],[10],[14],[5],[8],[12],[6],[1],[1],[8],[8],[3],[2],[2],[0],[1],[8],[5],[1],[7],[10],[7],[12],[14],[11],[8],[11],[13],[12],[12],[12],[13],[2],[4],[10],[12],[9],[6],[0],[5],[13],[12],[14],[1],[14],[9],[7],[12],[7],[10],[14],[10],[11],[14],[3],[8],[4],[9],[10],[5],[14],[6],[14],[5],[2],[8],[8],[6],[9],[11],[14],[3],[7],[9],[1],[2],[15],[2],[11],[2],[7],[5]],[[15],[2],[2],[8],[3],[9],[12],[15],[12],[11],[7],[10],[9],[1],[13],[10],[6],[7],[12],[3],[0],[8],[3],[4],[9],[6],[4],[12],[13],[9],[14],[10],[1],[13],[8],[1],[10],[3],[5],[4],[1],[2],[15],[9],[5],[8],[10],[11],[15],[15],[12],[6],[13],[2],[7],[1],[0],[5],[1],[1],[5],[9],[2],[14],[8],[0],[14],[7],[8],[2],[8],[12],[9],[12],[10],[2],[13],[6],[4],[10],[7],[7],[10],[0],[4],[14],[0],[10],[15],[10],[10],[12],[2],[6],[11],[8],[8],[5],[5],[3],[7],[9],[4],[14],[1],[8],[6],[10],[5],[12],[0],[0],[13],[9],[2],[1],[12],[13],[10],[10],[7],[10],[12],[1],[6],[3],[0],[5],[7],[13],[14],[11],[11],[13],[8],[8],[3],[4],[12],[7],[15],[14],[6],[6],[15],[2],[14],[7],[9],[6],[2],[3],[10],[1],[0],[9],[12],[11],[8],[13],[7],[15],[3],[4],[12],[11],[15],[8],[13],[11],[8],[7],[12],[11],[9],[0],[5],[5],[6],[12],[10],[3],[14],[10],[11],[4],[7],[12],[13],[0],[4],[10],[7],[15],[5],[2],[14],[12],[13],[7],[14],[9],[12],[15],[9],[8],[3],[6],[4],[13],[11],[15],[14],[13],[1],[3],[1],[9],[10],[2],[10],[0],[1],[11],[4],[13],[8],[3],[9],[11],[6],[0],[11],[6],[12],[9],[1],[3],[9],[9],[5],[15],[7],[2],[15],[7],[0],[2],[8],[5],[13],[11],[15],[5],[8],[15]],[[4],[9],[5],[14],[2],[3],[14],[8],[9],[7],[0],[9],[3],[3],[13],[4],[12],[9],[3],[13],[3],[11],[9],[11],[3],[9],[14],[3],[4],[0],[9],[4],[5],[1],[12],[13],[11],[13],[13],[13],[6],[9],[2],[10],[4],[9],[7],[8],[1],[10],[4],[0],[10],[9],[10],[4],[1],[3],[3],[10],[9],[2],[9],[15],[3],[4],[3],[15],[15],[3],[0],[5],[11],[1],[14],[13],[1],[2],[15],[10],[6],[6],[10],[9],[7],[7],[7],[7],[15],[1],[12],[8],[8],[5],[12],[4],[7],[14],[13],[4],[5],[7],[8],[12],[2],[15],[3],[8],[9],[12],[8],[1],[10],[11],[6],[5],[11],[7],[6],[10],[13],[3],[12],[8],[0],[1],[11],[3],[1],[3],[2],[2],[14],[14],[0],[13],[0],[13],[8],[2],[14],[3],[9],[0],[2],[1],[0],[0],[9],[8],[13],[9],[9],[11],[0],[13],[2],[6],[4],[6],[3],[8],[7],[13],[0],[13],[11],[2],[6],[7],[3],[13],[9],[7],[4],[3],[10],[4],[13],[6],[6],[5],[12],[2],[8],[11],[5],[8],[12],[6],[5],[11],[15],[15],[2],[3],[3],[7],[15],[10],[14],[10],[0],[0],[13],[1],[13],[10],[8],[6],[14],[6],[10],[0],[1],[4],[13],[1],[5],[10],[15],[4],[15],[11],[1],[13],[1],[8],[6],[4],[2],[3],[7],[12],[12],[1],[10],[1],[9],[15],[1],[11],[8],[14],[10],[15],[5],[8],[3],[2],[3],[12],[15],[3],[15],[15]],[[1],[6],[1],[2],[12],[2],[12],[10],[0],[6],[1],[9],[7],[7],[13],[5],[2],[14],[7],[14],[5],[8],[15],[3],[0],[9],[0],[6],[10],[12],[12],[4],[0],[5],[4],[7],[0],[10],[11],[3],[11],[5],[2],[7],[6],[8],[9],[11],[8],[11],[5],[11],[2],[9],[7],[1],[2],[14],[7],[2],[6],[0],[3],[11],[9],[13],[10],[4],[5],[4],[6],[12],[10],[2],[10],[5],[6],[1],[6],[6],[9],[6],[6],[11],[12],[14],[3],[5],[2],[5],[13],[11],[15],[15],[0],[11],[1],[3],[7],[7],[0],[12],[6],[15],[12],[9],[4],[12],[2],[14],[1],[9],[8],[6],[15],[12],[12],[6],[6],[8],[1],[1],[7],[2],[3],[12],[13],[4],[2],[3],[3],[5],[15],[10],[12],[1],[10],[2],[3],[14],[12],[8],[5],[6],[4],[14],[11],[1],[8],[9],[8],[3],[0],[15],[9],[14],[14],[15],[4],[5],[8],[7],[7],[2],[11],[7],[8],[14],[7],[1],[8],[0],[3],[2],[5],[6],[7],[2],[10],[6],[4],[10],[13],[5],[4],[3],[13],[11],[10],[11],[10],[3],[8],[5],[11],[1],[5],[12],[14],[10],[9],[12],[14],[8],[5],[10],[13],[9],[5],[13],[0],[5],[14],[11],[8],[9],[3],[9],[15],[14],[3],[13],[3],[6],[11],[2],[10],[4],[1],[1],[1],[9],[10],[8],[3],[6],[0],[13],[13],[2],[11],[3],[8],[13],[8],[6],[7],[5],[8],[15],[10],[0],[1],[0],[8],[3]],[[12],[5],[0],[7],[15],[11],[4],[7],[9],[11],[14],[4],[5],[3],[1],[0],[13],[2],[5],[14],[0],[9],[13],[7],[2],[5],[15],[7],[8],[5],[8],[12],[4],[13],[5],[5],[10],[11],[15],[3],[7],[12],[4],[6],[12],[7],[9],[11],[6],[6],[15],[11],[8],[2],[14],[14],[14],[14],[14],[3],[12],[8],[12],[1],[2],[9],[14],[3],[4],[3],[14],[9],[8],[7],[7],[10],[9],[7],[6],[11],[7],[2],[2],[13],[2],[6],[9],[6],[2],[6],[7],[6],[3],[3],[3],[6],[3],[5],[7],[3],[7],[12],[15],[14],[8],[13],[5],[1],[4],[4],[7],[9],[1],[3],[5],[13],[11],[15],[8],[15],[12],[14],[3],[3],[10],[9],[3],[3],[11],[2],[13],[1],[8],[10],[4],[5],[7],[10],[14],[1],[6],[12],[12],[12],[9],[10],[12],[12],[6],[11],[0],[4],[5],[0],[2],[0],[9],[6],[1],[5],[15],[2],[4],[4],[5],[6],[4],[8],[15],[9],[10],[0],[9],[4],[8],[4],[7],[4],[4],[1],[1],[9],[6],[12],[5],[14],[15],[1],[13],[0],[9],[0],[1],[13],[0],[6],[3],[14],[1],[3],[12],[0],[14],[4],[8],[14],[10],[13],[11],[11],[3],[15],[5],[0],[3],[8],[13],[7],[8],[8],[1],[11],[8],[2],[9],[1],[9],[0],[8],[11],[13],[15],[4],[6],[0],[12],[6],[13],[1],[15],[8],[6],[13],[9],[6],[1],[10],[15],[11],[1],[7],[9],[9],[7],[6],[2]]]
ZW = 278
def setup_inputs(rng):
    return {"z": rng.standard_normal((N, 128, ZW), dtype=np.float32), "g": rng.random((N, 128, T * K), dtype=np.float32)}
def reference(z, g):
    y = np.zeros((N, 128, T), np.float64)
    fill = [0] * N
    for r in range(N):
        for t in range(T):
            for k, e in enumerate(ROUTE[r][t]):
                y[r][:, t] += g[r][:, t * K + k].astype(np.float64) * z[e][:, fill[e]].astype(np.float64)
                fill[e] += 1
    return {"y": y.astype(z.dtype)}

@@ -1,0 +1,78 @@
+from concourse.mybir import AluOpType
+
+SCRATCH = {
+    "zbuf": ("sbuf", [128, 278], "float32"),
+    "gbuf": ("sbuf", [128, 256], "float32"),
+    "land": ("sbuf", [128, 256], "float32"),
+    "ybuf": ("sbuf", [128, 256], "float32"),
+}
+SEMAPHORES = ["zl", "gl", "sent", "arrived", "done", "stored"]
+
+
+def plan(route, n):
+    toks = [[[t for t in range(len(route[r])) if route[r][t][0] == e] for e in range(n)] for r in range(n)]
+    cnt = [[len(toks[r][e]) for r in range(n)] for e in range(n)]
+    zoff = [[sum(cnt[e][:r]) for r in range(n)] for e in range(n)]
+    loff = [[sum(cnt[x][r] for x in range(e)) for e in range(n)] for r in range(n)]
+    return toks, cnt, zoff, loff
+
+
+def runs(ts):
+    out = []
+    i = 0
+    while i < len(ts):
+        if i + 1 == len(ts):
+            out.append((i, 1, 1))
+            break
+        s = ts[i + 1] - ts[i]
+        j = i + 1
+        while j + 1 < len(ts) and ts[j + 1] - ts[j] == s:
+            j += 1
+        out.append((i, j - i + 1, s))
+        i = j + 1
+    return out
+
+
+def rank_program(g, core, T, topo):
+    me = T.rank_of(core)
+    if me is None:
+        return
+    n = len(T.cores)
+    toks, cnt, zoff, loff = plan(T.tables["ROUTE"], n)
+
+    g.sync.dma_start(T.zbuf[:], T.z[:]).then_inc(T.sem.zl, 16)
+    g.scalar.dma_start(T.gbuf[:], T.g[:]).then_inc(T.sem.gl, 16)
+
+    g.wait_ge(T.sem.zl, 16)
+    sent = 0
+    for d in range(1, n):
+        r = (me + d) % n
+        c = cnt[me][r]
+        if c == 0:
+            continue
+        dst = T.cores[r]
+        rid, pid, _se = topo.addr(dst)
+        g.remote_dma(T.land[:, loff[r][me]:loff[r][me] + c], T.zbuf[:, zoff[me][r]:zoff[me][r] + c],
+                     T.sem.arrived, T.sem.sent, pid, rid, topo.mask(core, dst))
+        sent += 8
+
+    v = g.vector
+    arrive = 8 * sum(1 for e in range(n) if e != me and cnt[e][me] > 0)
+    v.wait_ge(T.sem.zl, 16)
+    v.wait_ge(T.sem.gl, 16)
+    v.wait_ge(T.sem.arrived, arrive)
+    ops = 0
+    for e in range(n):
+        ts = toks[me][e]
+        src, base = (T.zbuf, zoff[me][me]) if e == me else (T.land, loff[me][e])
+        for i, m, s in runs(ts):
+            t0 = ts[i]
+            sl = slice(t0, t0 + (m - 1) * s + 1, s)
+            v.tensor_tensor(out=T.ybuf[:, sl], in0=src[:, base + i:base + i + m], in1=T.gbuf[:, sl],
+                            op=AluOpType.mult).then_inc(T.sem.done, 1)
+            ops += 1
+
+    g.sync.wait_ge(T.sem.done, ops)
+    g.sync.dma_start(T.y[:], T.ybuf[:]).then_inc(T.sem.stored, 16)
+    g.sync.wait_ge(T.sem.stored, 16)
+    g.wait_ge(T.sem.sent, sent)

@@ -8,11 +8,19 @@ SCRATCH = {
 }
 SEMAPHORES = ["zl", "gl", "sent", "arrived", "done", "stored"]
 
+HELPERS = (2, 3, 7)
+VIA = (
+    ((4, 7), (12, 16), (7, 11)), ((4, 8), (12, 16), (8, 11)), ((5, 9), (13, 16), (9, 13)), ((4, 8), (13, 16), (8, 12)),
+    ((0, 4), (8, 12), (5, 8)), ((0, 4), (12, 16), (6, 9)), ((0, 3), (12, 16), (7, 11)), ((2, 5), (8, 12), (12, 16)),
+    ((3, 7), (13, 16), (9, 13)), ((4, 8), (10, 13), (0, 4)), ((0, 4), (7, 10), (11, 15)), ((3, 7), (8, 11), (12, 16)),
+    ((0, 4), (9, 12), (4, 8)), ((5, 9), (10, 13), (0, 4)), ((0, 4), (9, 13), (4, 7)), ((0, 4), (9, 12), (4, 8)),
+)
+
 
 def plan(route, n):
     toks = [[[t for t in range(len(route[r])) if route[r][t][0] == e] for e in range(n)] for r in range(n)]
     cnt = [[len(toks[r][e]) for r in range(n)] for e in range(n)]
-    zoff = [[sum(cnt[e][:r]) for r in range(n)] for e in range(n)]
+    zoff = [[sum(cnt[e][:r]) for r in range(n + 1)] for e in range(n)]
     loff = [[sum(cnt[x][r] for x in range(e)) for e in range(n)] for r in range(n)]
     return toks, cnt, zoff, loff
 
@@ -34,40 +42,63 @@ def runs(ts):
 
 
 def rank_program(g, core, T, topo):
-    me = T.rank_of(core)
-    if me is None:
-        return
     n = len(T.cores)
     toks, cnt, zoff, loff = plan(T.tables["ROUTE"], n)
+    expert_on = {topo.chip(c): e for e, c in enumerate(T.cores)}
+    me = T.rank_of(core)
+
+    def forward(e, ranks):
+        added = 0
+        for r in ranks:
+            c = cnt[e][r]
+            if c == 0:
+                continue
+            dst = T.cores[r]
+            rid, pid, _se = topo.addr(dst)
+            g.remote_dma(T.land[:, loff[r][e]:loff[r][e] + c], T.zbuf[:, zoff[e][r]:zoff[e][r] + c],
+                         T.sem.arrived, T.sem.sent, pid, rid, topo.mask(core, dst))
+            added += 8
+        return added
+
+    if me is None:
+        e = expert_on.get(topo.chip(core))
+        k = core % 8
+        if e is None or k not in HELPERS:
+            return
+        a, b = VIA[e][HELPERS.index(k)]
+        if zoff[e][b] == zoff[e][a]:
+            return
+        g.wait_ge(T.sem.arrived, 16)
+        g.wait_ge(T.sem.sent, forward(e, range(a, b)))
+        return
 
     g.sync.dma_start(T.zbuf[:], T.z[:]).then_inc(T.sem.zl, 16)
     g.scalar.dma_start(T.gbuf[:], T.g[:]).then_inc(T.sem.gl, 16)
 
     g.wait_ge(T.sem.zl, 16)
     sent = 0
-    for d in range(1, n):
-        r = (me + d) % n
-        c = cnt[me][r]
-        if c == 0:
+    mine = [r for r in range(n) if r != me]
+    for k, (a, b) in zip(HELPERS, VIA[me]):
+        mine = [r for r in mine if not a <= r < b]
+        lo, hi = zoff[me][a], zoff[me][b]
+        if hi == lo:
             continue
-        dst = T.cores[r]
+        dst = core - core % 8 + k
         rid, pid, _se = topo.addr(dst)
-        g.remote_dma(T.land[:, loff[r][me]:loff[r][me] + c], T.zbuf[:, zoff[me][r]:zoff[me][r] + c],
-                     T.sem.arrived, T.sem.sent, pid, rid, topo.mask(core, dst))
-        sent += 8
+        g.remote_dma(T.zbuf[:, lo:hi], T.zbuf[:, lo:hi], T.sem.arrived, T.sem.sent, pid, rid, topo.mask(core, dst))
+        sent += 16
+    sent += forward(me, mine)
 
     v = g.vector
-    arrive = 8 * sum(1 for e in range(n) if e != me and cnt[e][me] > 0)
     v.wait_ge(T.sem.zl, 16)
     v.wait_ge(T.sem.gl, 16)
-    v.wait_ge(T.sem.arrived, arrive)
+    v.wait_ge(T.sem.arrived, 8 * sum(1 for e in range(n) if e != me and cnt[e][me] > 0))
     ops = 0
     for e in range(n):
         ts = toks[me][e]
         src, base = (T.zbuf, zoff[me][me]) if e == me else (T.land, loff[me][e])
         for i, m, s in runs(ts):
-            t0 = ts[i]
-            sl = slice(t0, t0 + (m - 1) * s + 1, s)
+            sl = slice(ts[i], ts[i] + (m - 1) * s + 1, s)
             v.tensor_tensor(out=T.ybuf[:, sl], in0=src[:, base + i:base + i + m], in1=T.gbuf[:, sl],
                             op=AluOpType.mult).then_inc(T.sem.done, 1)
             ops += 1

from concourse.mybir import AluOpType

SCRATCH = {
    "zbuf": ("sbuf", [128, 278], "float32"),
    "gbuf": ("sbuf", [128, 256], "float32"),
    "land": ("sbuf", [128, 256], "float32"),
    "ybuf": ("sbuf", [128, 256], "float32"),
}
SEMAPHORES = ["zl", "gl", "sent", "arrived", "done", "stored"]

HELPERS = (2, 3, 7)
VIA = (
    ((4, 7), (12, 16), (7, 11)), ((4, 8), (12, 16), (8, 11)), ((5, 9), (13, 16), (9, 13)), ((4, 8), (13, 16), (8, 12)),
    ((0, 4), (8, 12), (5, 8)), ((0, 4), (12, 16), (6, 9)), ((0, 3), (12, 16), (7, 11)), ((2, 5), (8, 12), (12, 16)),
    ((3, 7), (13, 16), (9, 13)), ((4, 8), (10, 13), (0, 4)), ((0, 4), (7, 10), (11, 15)), ((3, 7), (8, 11), (12, 16)),
    ((0, 4), (9, 12), (4, 8)), ((5, 9), (10, 13), (0, 4)), ((0, 4), (9, 13), (4, 7)), ((0, 4), (9, 12), (4, 8)),
)


def plan(route, n):
    toks = [[[t for t in range(len(route[r])) if route[r][t][0] == e] for e in range(n)] for r in range(n)]
    cnt = [[len(toks[r][e]) for r in range(n)] for e in range(n)]
    zoff = [[sum(cnt[e][:r]) for r in range(n + 1)] for e in range(n)]
    loff = [[sum(cnt[x][r] for x in range(e)) for e in range(n)] for r in range(n)]
    return toks, cnt, zoff, loff


def runs(ts):
    out = []
    i = 0
    while i < len(ts):
        if i + 1 == len(ts):
            out.append((i, 1, 1))
            break
        s = ts[i + 1] - ts[i]
        j = i + 1
        while j + 1 < len(ts) and ts[j + 1] - ts[j] == s:
            j += 1
        out.append((i, j - i + 1, s))
        i = j + 1
    return out


def rank_program(g, core, T, topo):
    n = len(T.cores)
    toks, cnt, zoff, loff = plan(T.tables["ROUTE"], n)
    expert_on = {topo.chip(c): e for e, c in enumerate(T.cores)}
    me = T.rank_of(core)

    def forward(e, ranks):
        added = 0
        for r in ranks:
            c = cnt[e][r]
            if c == 0:
                continue
            dst = T.cores[r]
            rid, pid, _se = topo.addr(dst)
            g.remote_dma(T.land[:, loff[r][e]:loff[r][e] + c], T.zbuf[:, zoff[e][r]:zoff[e][r] + c],
                         T.sem.arrived, T.sem.sent, pid, rid, topo.mask(core, dst))
            added += 8
        return added

    if me is None:
        e = expert_on.get(topo.chip(core))
        k = core % 8
        if e is None or k not in HELPERS:
            return
        a, b = VIA[e][HELPERS.index(k)]
        if zoff[e][b] == zoff[e][a]:
            return
        g.wait_ge(T.sem.arrived, 16)
        g.wait_ge(T.sem.sent, forward(e, range(a, b)))
        return

    g.sync.dma_start(T.zbuf[:], T.z[:]).then_inc(T.sem.zl, 16)
    g.scalar.dma_start(T.gbuf[:], T.g[:]).then_inc(T.sem.gl, 16)

    g.wait_ge(T.sem.zl, 16)
    sent = 0
    mine = [r for r in range(n) if r != me]
    for k, (a, b) in zip(HELPERS, VIA[me]):
        mine = [r for r in mine if not a <= r < b]
        lo, hi = zoff[me][a], zoff[me][b]
        if hi == lo:
            continue
        dst = core - core % 8 + k
        rid, pid, _se = topo.addr(dst)
        g.remote_dma(T.zbuf[:, lo:hi], T.zbuf[:, lo:hi], T.sem.arrived, T.sem.sent, pid, rid, topo.mask(core, dst))
        sent += 16
    sent += forward(me, mine)

    v = g.vector
    v.wait_ge(T.sem.zl, 16)
    v.wait_ge(T.sem.gl, 16)
    v.wait_ge(T.sem.arrived, 8 * sum(1 for e in range(n) if e != me and cnt[e][me] > 0))
    ops = 0
    for e in range(n):
        ts = toks[me][e]
        src, base = (T.zbuf, zoff[me][me]) if e == me else (T.land, loff[me][e])
        for i, m, s in runs(ts):
            sl = slice(ts[i], ts[i] + (m - 1) * s + 1, s)
            v.tensor_tensor(out=T.ybuf[:, sl], in0=src[:, base + i:base + i + m], in1=T.gbuf[:, sl],
                            op=AluOpType.mult).then_inc(T.sem.done, 1)
            ops += 1

    g.sync.wait_ge(T.sem.done, ops)
    g.sync.dma_start(T.y[:], T.ybuf[:]).then_inc(T.sem.stored, 16)
    g.sync.wait_ge(T.sem.stored, 16)
    g.wait_ge(T.sem.sent, sent)
